import numpy as np
import ml_dtypes


def mxq(x, axis, fmt="e4m3"):
    dtype, down = {"e4m3": (ml_dtypes.float8_e4m3fn, 7), "e5m2": (ml_dtypes.float8_e5m2, 14)}[fmt]
    v = np.moveaxis(np.asarray(x, np.float32).astype(ml_dtypes.bfloat16).astype(np.float64), axis, -1)
    blocks = v.reshape(v.shape[:-1] + (-1, 32))
    amax = np.abs(blocks).max(-1, keepdims=True)
    byte = np.maximum(np.where(amax > 0, np.frexp(amax)[1] - 1 + 127, 0) - down, 1)
    scale = np.exp2(byte - 127.0)
    codes = (blocks / scale).astype(np.float32).astype(dtype).astype(np.float64)
    return np.moveaxis((codes * scale).reshape(v.shape), -1, axis)


WIDE = False


def mx_kscale(k):
    if not WIDE:
        return np.ones(k)
    levels = np.array([10, -10, 5, -5, 0])
    if k % 512:
        return np.exp2(np.random.permutation(np.resize(levels, k // 32))).repeat(32)
    a = np.empty((k // 512, 16))
    for p in range(k // 512):
        a[p, :8] = np.random.permutation(np.resize(levels, 8))
        for g in range(8):
            far = levels[np.abs(levels - a[p, g]) >= 10]
            a[p, g + 8] = far[np.random.randint(len(far))]
    return np.exp2(a.ravel()).repeat(32)


def f64(x):
    return np.asarray(x).astype(np.float64)


def striped(idx):
    return np.tile(idx.reshape(-1, 16).T, (8, 1)).astype(np.uint16)


def unstriped(offs):
    return offs[:16].T.reshape(-1).astype(np.int64)


E2M1 = np.array([0.0, 0.5, 1.0, 1.5, 2.0, 3.0, 4.0, 6.0, -0.0, -0.5, -1.0, -1.5, -2.0, -3.0, -4.0, -6.0])


def pack_weight(w, fmt):
    k, n = w.shape
    w = f64(np.asarray(w, np.float32).astype(ml_dtypes.bfloat16)).reshape(k // 32, 32, n)
    amax = np.abs(w).max(1)
    if fmt == "e4m3":
        byte = np.frexp(amax)[1] - 1 + 127 - 7
    else:
        mant, ex = np.frexp(amax / 6.0)
        byte = np.where(mant > 0.5, ex, ex - 1) + 127
    byte = np.clip(np.where(amax > 0, byte, 1), 1, 254)
    scaled = (w * np.exp2(127.0 - byte)[:, None, :]).reshape(k, n).astype(np.float32)
    by_word = np.ascontiguousarray(scaled.reshape(k // 512, 128, 4, n).transpose(0, 1, 3, 2))
    if fmt == "e4m3":
        words = by_word.astype(ml_dtypes.float8_e4m3fn).view(np.uint8)
    else:
        c = by_word.astype(ml_dtypes.float4_e2m1fn).view(np.uint8) & 0xF
        words = (c[..., 0::2] | (c[..., 1::2] << 4)).reshape(k // 512, 128, 2 * n)
    return np.ascontiguousarray(words), np.ascontiguousarray(byte.astype(np.uint8).reshape(k // 512, 16, n))


def unpack_weight(words, scales, fmt):
    g, _, n = scales.shape
    words = np.ascontiguousarray(words).reshape(g, 128, n, -1)
    if fmt == "e4m3":
        vals = words.view(ml_dtypes.float8_e4m3fn).astype(np.float64)
    else:
        nib = np.empty((g, 128, n, 4), np.uint8)
        nib[..., 0::2] = words & 0xF
        nib[..., 1::2] = words >> 4
        vals = E2M1[nib]
    vals = vals * np.repeat(np.exp2(scales.astype(np.float64) - 127.0), 8, axis=1)[..., None]
    return vals.transpose(0, 1, 3, 2).reshape(g * 512, n)


def silu(v):
    return v / (1.0 + np.exp(-np.maximum(v, -700.0)))


K, L, T, Q, E, C, D = 512, 512, 512, 1024, 2, 256, 256
H, N = 512, 512


def by_expert(wq, xq, C):
    return np.concatenate([wq[e].T @ xq[:, e * C:(e + 1) * C] for e in range(E)], axis=1)


def setup_inputs():
    n = np.random.standard_normal
    s = mx_kscale(K)
    v = mx_kscale(L)
    u = mx_kscale(H)
    slots1, slots2 = np.random.permutation(T)[:E * C], np.random.permutation(Q)[:E * D]
    x = pack_weight(n((K, T)) * s[:, None], "e4m3")
    z = pack_weight(n((L, Q)) * v[:, None], "e4m3")
    w1 = [pack_weight(m, "e2m1") for m in n((E, K, H)) / np.sqrt(K) / s[None, :, None] * u]
    w2 = [pack_weight(m, "e2m1") for m in n((E, H, N)) / np.sqrt(H) / u[None, :, None]]
    return {
        "x_words": x[0],
        "x_scales": x[1],
        "z_words": z[0],
        "z_scales": z[1],
        "w1_words": np.stack([m[0] for m in w1]),
        "w1_scales": np.stack([m[1] for m in w1]),
        "wz": (n((E, L, H)) / np.sqrt(L) / v[None, :, None] * u).astype(np.float32),
        "w2_words": np.stack([m[0] for m in w2]),
        "w2_scales": np.stack([m[1] for m in w2]),
        "gate1": (np.tile(np.random.uniform(0.2, 1.0, E * C), (128, 1))).astype(np.float32),
        "gate2": (np.tile(np.random.uniform(0.2, 1.0, E * D), (128, 1))).astype(np.float32),
        "offs": striped(slots1),
        "offs2": striped(slots2),
    }


def reference(x_words, x_scales, z_words, z_scales, w1_words, w1_scales, wz, w2_words, w2_scales, gate1, gate2, offs, offs2):
    w1 = np.stack([unpack_weight(w1_words[e], w1_scales[e], "e2m1") for e in range(E)])
    wzq = mxq(f64(wz), 1, "e4m3")
    w2 = np.stack([unpack_weight(w2_words[e], w2_scales[e], "e2m1") for e in range(E)])
    idx, idx2 = unstriped(offs), unstriped(offs2)
    xq = unpack_weight(x_words, x_scales, "e4m3")[:, idx]
    zq = unpack_weight(z_words, z_scales, "e4m3")[:, idx2]
    h = silu(by_expert(w1, xq, C))
    p = silu(by_expert(wzq, zq, D))
    out = np.zeros((N, T + Q))
    out[:, idx] = f64(gate1[:1]) * by_expert(w2, mxq(h, 0, "e4m3"), C)
    out[:, T + idx2] = f64(gate2[:1]) * by_expert(w2, mxq(p, 0, "e4m3"), D)
    return out

@@ -1,0 +1,203 @@
+from contextlib import ExitStack
+
+import concourse.mybir as mybir
+
+F32 = mybir.dt.float32
+BF16 = mybir.dt.bfloat16
+I32 = mybir.dt.int32
+U32 = mybir.dt.uint32
+U16 = mybir.dt.uint16
+U8 = mybir.dt.uint8
+FP8X4 = mybir.dt.float8_e4m3fn_x4
+FP4X4 = mybir.dt.float4_e2m1fn_x4
+SILU = mybir.ActivationFunctionType.Silu
+MULT = mybir.AluOpType.mult
+
+P = 128
+PACK = 4
+E = 2
+SLOTS = 256
+T = 512
+Q = 1024
+H = 512
+N = 512
+GROUP = 128
+BLOCKS = N // P
+LIST_COLS = SLOTS // 16
+PATCH_WINDOWS = 3
+
+FLOPS = 1073741824
+
+
+def tile_moe_mmo_silu_kernel(
+    tc, x_words, x_scales, z_words, z_scales, w1_words, w1_scales, wz, w2_words, w2_scales,
+    gate1, gate2, offs, offs2, out,
+):
+    nc = tc.nc
+    with ExitStack() as ctx:
+        keep = ctx.enter_context(tc.tile_pool(name="keep", bufs=1))
+        psum = ctx.enter_context(tc.psum_pool(name="psum", bufs=1))
+
+        def sb(name, shape, dtype, tag=None):
+            return keep.tile(shape, dtype, name=name, tag=tag or name, align_bytes=64)
+
+        def bank(name, b):
+            return psum.tile([P, 512], F32, name=name, tag="bank%d" % b)
+
+        text_list = keep.tile([P, T // 16], U16, name="text_list")
+        patch_list = keep.tile([P, T // 16], U16, name="patch_list")
+        x_win = sb("x_win", [P, T], I32)
+        z_win = sb("z_win", [P, Q], I32)
+        xs_win = sb("xs_win", [P, T], U8)
+        zs_win = sb("zs_win", [P, Q], U8)
+        w1_raw = sb("w1_raw", [P, E, 2 * H], U8)
+        w1s_raw = sb("w1s_raw", [P, E, H], U8)
+        w2_codes = sb("w2_codes", [P, E, 2 * N], U8)
+        w2_plane = sb("w2_plane", [P, E, N], U8)
+        g1 = sb("g1", [P, E * SLOTS], F32)
+        g2 = sb("g2", [P, E * SLOTS], F32)
+        wz_raw = [sb("wz_raw%d" % e, [P, PACK, H], F32) for e in range(E)]
+        text_out = [sb("text_out%d" % b, [P, T], F32) for b in range(BLOCKS)]
+        patch_out = [sb("patch_out%d" % w, [P, Q], F32) for w in range(PATCH_WINDOWS)]
+
+        nc.vector.memset(xs_win[:].bitcast(I32), 0)
+        nc.vector.memset(w1s_raw[:].rearrange("p e c -> p (e c)").bitcast(I32), 0)
+        nc.vector.memset(zs_win[:].bitcast(I32), 0)
+        nc.vector.memset(w2_plane[:].rearrange("p e c -> p (e c)").bitcast(I32), 0)
+        for w in range(PATCH_WINDOWS):
+            nc.gpsimd.memset(patch_out[w][:], 0.0)
+
+        def load_token_scales(plane, scales):
+            rows = scales[0].rearrange("(q r) t -> r q t", r=4)
+            for r in range(4):
+                nc.sync.dma_start(plane[r:P:32, :].bitcast(I32), rows[r].bitcast(I32))
+
+        def load_weight_scales(plane, scales):
+            rows = scales.rearrange("e s (q r) c -> r q (e s) c", r=4)
+            for r in range(4):
+                nc.sync.dma_start(plane[r:P:32, :, :].bitcast(I32), rows[r].bitcast(I32))
+
+        def load_weight_words(tile, words):
+            nc.sync.dma_start(tile[:].bitcast(I32), words.rearrange("e s p b -> p (e s) b").bitcast(I32))
+
+        def load_token_words(tile, words):
+            nc.sync.dma_start(tile[:], words[0].rearrange("p t d -> p (t d)").bitcast(I32))
+
+        nc.sync.dma_start(text_list[:], offs)
+        load_token_words(x_win, x_words)
+        load_token_scales(xs_win, x_scales)
+        load_weight_words(w1_raw, w1_words)
+        load_weight_scales(w1s_raw, w1_scales)
+        nc.sync.dma_start(patch_list[:], offs2)
+        load_token_words(z_win, z_words)
+        load_token_scales(zs_win, z_scales)
+        load_weight_words(w2_codes, w2_words)
+        load_weight_scales(w2_plane, w2_scales)
+        nc.sync.dma_start(g1[:], gate1)
+        for e in range(E):
+            nc.sync.dma_start(wz_raw[e][:], wz[e].rearrange("(p j) c -> p j c", j=PACK))
+        nc.sync.dma_start(g2[:], gate2)
+
+        def gather(name, words, plane, offsets, count):
+            got = sb(name + "_words", [P, count], U32)
+            got_plane = sb(name + "_plane", [P, count], U8)
+            nc.vector.tensor_copy(got[:], words[:].bitcast(U32).indirect(offsets))
+            nc.vector.tensor_copy(got_plane[:], plane[:].indirect(offsets))
+            return got, got_plane
+
+        def permute_w1(e):
+            codes = sb("w1_codes%d" % e, [P, 2 * H], U8)
+            plane = sb("w1_plane%d" % e, [P, H], U8)
+            nc.vector.tensor_copy(
+                codes[:].bitcast(U16).rearrange("p (t a m) -> p a t m", t=PACK, m=8),
+                w1_raw[:, e, :].bitcast(U16).rearrange("p (a m t) -> p a t m", t=PACK, m=8),
+            )
+            nc.vector.tensor_copy(
+                plane[:].rearrange("p (t a m) -> p a t m", t=PACK, m=16),
+                w1s_raw[:, e, :].rearrange("p (a m t) -> p a t m", t=PACK, m=16),
+            )
+            return (lambda t: codes[:, 2 * P * t : 2 * P * (t + 1)].bitcast(FP4X4)), plane
+
+        def first_layer(name, weights, w_plane, tokens, t_plane, col, banks):
+            hidden = sb(name + "_hidden", [P, SLOTS * PACK], BF16)
+            for g in range(SLOTS // GROUP):
+                acc = bank("%s_acc%d" % (name, g), banks[g])
+                cols = slice(col + g * GROUP, col + (g + 1) * GROUP)
+                for t in range(PACK):
+                    nc.tensor.matmul_mx(
+                        acc[:, t * GROUP : (t + 1) * GROUP],
+                        lhsT=weights(t), lhsT_scale=w_plane[:, t * P : (t + 1) * P],
+                        rhs=tokens[:, cols].bitcast(FP8X4), rhs_scale=t_plane[:, cols],
+                        start=True, stop=True,
+                    )
+                nc.scalar.activation(
+                    hidden[:, g * GROUP * PACK : (g + 1) * GROUP * PACK].rearrange("p (n t) -> p n t", t=PACK),
+                    acc[:].rearrange("p (t n) -> p n t", t=PACK), SILU,
+                )
+            codes = sb(name + "_hcodes", [P, SLOTS], U32)
+            plane = sb(name + "_hplane", [P, SLOTS], U8)
+            nc.vector.quantize_mx(codes[:].bitcast(FP8X4), plane[:], hidden[:])
+            return codes, plane
+
+        def second_matmul(acc, e, b, hidden):
+            codes, plane = hidden
+            nc.tensor.matmul_mx(
+                acc,
+                lhsT=w2_codes[:, e, 2 * P * b : 2 * P * (b + 1)].bitcast(FP4X4),
+                lhsT_scale=w2_plane[:, e, P * b : P * (b + 1)],
+                rhs=codes[:].bitcast(FP8X4), rhs_scale=plane[:],
+                start=True, stop=True,
+            )
+
+        def text_block(e, b, hidden, bank_no, tag=None):
+            acc = bank("text_acc%d_%d" % (e, b), bank_no)
+            second_matmul(acc[:, 0:SLOTS], e, b, hidden)
+            staged = sb("text_staged%d_%d" % (e, b), [P, SLOTS], F32, tag)
+            nc.scalar.copy(staged[:], acc[:, 0:SLOTS])
+            nc.vector.tensor_tensor(
+                text_out[b][:].indirect(text_list[:, e * LIST_COLS : (e + 1) * LIST_COLS]),
+                staged[:], g1[:, e * SLOTS : (e + 1) * SLOTS], MULT,
+            )
+            if e == E - 1:
+                nc.sync.dma_start(out[b * P : (b + 1) * P, 0:T], text_out[b][:])
+
+        def patch_block(b, hidden, bank_no):
+            acc = bank("patch_acc%d" % b, bank_no)
+            for e in range(E):
+                second_matmul(acc[:, e * SLOTS : (e + 1) * SLOTS], e, b, hidden[e])
+            staged = sb("patch_staged%d" % b, [P, E * SLOTS], F32)
+            nc.scalar.copy(staged[:], acc[:])
+            window = patch_out[b % PATCH_WINDOWS]
+            nc.vector.tensor_tensor(window[:].indirect(patch_list[:]), staged[:], g2[:], MULT)
+            nc.sync.dma_start(out[b * P : (b + 1) * P, T : T + Q], window[:])
+
+        def quantize_wz(e):
+            grouped = sb("wz_grouped%d" % e, [P, H * PACK], BF16)
+            nc.scalar.copy(
+                grouped[:].rearrange("p (t m j) -> p m t j", t=PACK, j=PACK),
+                wz_raw[e][:].rearrange("p j (m t) -> p m t j", t=PACK),
+            )
+            codes = sb("wz_codes%d" % e, [P, H], U32)
+            plane = sb("wz_plane%d" % e, [P, H], U8)
+            nc.vector.quantize_mx(codes[:].bitcast(FP8X4), plane[:], grouped[:])
+            return (lambda t: codes[:, P * t : P * (t + 1)].bitcast(FP8X4)), plane
+
+        text_hidden = []
+        for e in range(E):
+            tokens, t_plane = gather("x%d" % e, x_win, xs_win, text_list[:, e * LIST_COLS : (e + 1) * LIST_COLS], SLOTS)
+            weights, w_plane = permute_w1(e)
+            text_hidden.append(first_layer("text%d" % e, weights, w_plane, tokens, t_plane, 0, (2 * e, 2 * e + 1)))
+        patches, p_plane = gather("z", z_win, zs_win, patch_list[:], E * SLOTS)
+        for b in range(BLOCKS):
+            text_block(0, b, text_hidden[0], 4 + b)
+        text_block(1, 0, text_hidden[1], 0)
+        wz_q = [quantize_wz(e) for e in range(E)]
+        text_block(1, 1, text_hidden[1], 1, "wz_raw0")
+        patch_hidden = [
+            first_layer("patch%d" % e, wz_q[e][0], wz_q[e][1], patches, p_plane, e * SLOTS, (2 + 2 * e, 3 + 2 * e))
+            for e in range(E)
+        ]
+        text_block(1, 2, text_hidden[1], 2)
+        for b in range(BLOCKS):
+            patch_block(b, patch_hidden, (6, 7, 0, 1)[b])
+        text_block(1, 3, text_hidden[1], 1)

@@ -1,6 +1,7 @@
 from contextlib import ExitStack
 
 import concourse.mybir as mybir
+from concourse.masks import make_identity
 
 F32 = mybir.dt.float32
 BF16 = mybir.dt.bfloat16
@@ -24,7 +25,6 @@ N = 512
 GROUP = 128
 BLOCKS = N // P
 LIST_COLS = SLOTS // 16
-PATCH_WINDOWS = 3
 
 FLOPS = 1073741824
 
@@ -56,16 +56,21 @@ def tile_moe_mmo_silu_kernel(
         w2_plane = sb("w2_plane", [P, E, N], U8)
         g1 = sb("g1", [P, E * SLOTS], F32)
         g2 = sb("g2", [P, E * SLOTS], F32)
-        wz_raw = [sb("wz_raw%d" % e, [P, PACK, H], F32) for e in range(E)]
+        wz_raw = [[sb("wz_raw%d_%d" % (e, h), [P, PACK, H // 2], F32) for h in range(2)] for e in range(E)]
         text_out = [sb("text_out%d" % b, [P, T], F32) for b in range(BLOCKS)]
-        patch_out = [sb("patch_out%d" % w, [P, Q], F32) for w in range(PATCH_WINDOWS)]
+        patch_out = [sb("patch_out%d" % b, [P, Q], F32) for b in range(BLOCKS)]
 
         nc.vector.memset(xs_win[:].bitcast(I32), 0)
         nc.vector.memset(w1s_raw[:].rearrange("p e c -> p (e c)").bitcast(I32), 0)
         nc.vector.memset(zs_win[:].bitcast(I32), 0)
         nc.vector.memset(w2_plane[:].rearrange("p e c -> p (e c)").bitcast(I32), 0)
-        for w in range(PATCH_WINDOWS):
-            nc.gpsimd.memset(patch_out[w][:], 0.0)
+        warm = sb("warm", [P, 2], F32)
+        nc.vector.memset(warm[:, 0:1], 0.0)
+        nc.scalar.activation(warm[:, 1:2], warm[:, 0:1], SILU)
+        identity = sb("identity", [P, P], F32)
+        make_identity(nc, identity[:])
+        for b in range(BLOCKS):
+            nc.gpsimd.memset(patch_out[b][:], 0.0)
 
         def load_token_scales(plane, scales):
             rows = scales[0].rearrange("(q r) t -> r q t", r=4)
@@ -91,11 +96,14 @@ def tile_moe_mmo_silu_kernel(
         nc.sync.dma_start(patch_list[:], offs2)
         load_token_words(z_win, z_words)
         load_token_scales(zs_win, z_scales)
-        load_weight_words(w2_codes, w2_words)
         load_weight_scales(w2_plane, w2_scales)
+        load_weight_words(w2_codes, w2_words)
         nc.sync.dma_start(g1[:], gate1)
         for e in range(E):
-            nc.sync.dma_start(wz_raw[e][:], wz[e].rearrange("(p j) c -> p j c", j=PACK))
+            for h in range(2):
+                nc.sync.dma_start(
+                    wz_raw[e][h][:], wz[e][:, h * H // 2 : (h + 1) * H // 2].rearrange("(p j) c -> p j c", j=PACK)
+                )
         nc.sync.dma_start(g2[:], gate2)
 
         def gather(name, words, plane, offsets, count):
@@ -105,21 +113,31 @@ def tile_moe_mmo_silu_kernel(
             nc.vector.tensor_copy(got_plane[:], plane[:].indirect(offsets))
             return got, got_plane
 
-        def permute_w1(e):
-            codes = sb("w1_codes%d" % e, [P, 2 * H], U8)
-            plane = sb("w1_plane%d" % e, [P, H], U8)
-            nc.vector.tensor_copy(
-                codes[:].bitcast(U16).rearrange("p (t a m) -> p a t m", t=PACK, m=8),
-                w1_raw[:, e, :].bitcast(U16).rearrange("p (a m t) -> p a t m", t=PACK, m=8),
+        def text_first_layer(e, g, tokens, t_plane, hidden, acc_bank, turn_bank):
+            cols = slice(g * GROUP, (g + 1) * GROUP)
+            acc = bank("text_acc1_%d_%d" % (e, g), acc_bank)
+            nc.tensor.matmul_mx(
+                acc[:],
+                lhsT=tokens[:, cols].bitcast(FP8X4), lhsT_scale=t_plane[:, cols],
+                rhs=w1_raw[:, e, :].bitcast(FP4X4), rhs_scale=w1s_raw[:, e, :],
+                start=True, stop=True,
             )
-            nc.vector.tensor_copy(
-                plane[:].rearrange("p (t a m) -> p a t m", t=PACK, m=16),
-                w1s_raw[:, e, :].rearrange("p (a m t) -> p a t m", t=PACK, m=16),
+            by_slot = sb("text_by_slot%d_%d" % (e, g), [P, H], BF16)
+            nc.scalar.activation(
+                by_slot[:].rearrange("s (u p b) -> s u p b", u=2, b=2),
+                acc[:].rearrange("s (p u b) -> s u p b", u=2, b=2), SILU,
             )
-            return (lambda t: codes[:, 2 * P * t : 2 * P * (t + 1)].bitcast(FP4X4)), plane
+            turned = bank("text_turned%d_%d" % (e, g), turn_bank)
+            for u in range(2):
+                nc.tensor.transpose(
+                    turned[:, u * P : (u + 1) * P], by_slot[:].bitcast(F32)[:, u * P : (u + 1) * P], identity[:]
+                )
+            nc.scalar.copy(
+                hidden.bitcast(F32).rearrange("p (s u) -> p s u", u=2),
+                turned[:, 0 : 2 * P].rearrange("p (u s) -> p s u", u=2),
+            )
 
-        def first_layer(name, weights, w_plane, tokens, t_plane, col, banks):
-            hidden = sb(name + "_hidden", [P, SLOTS * PACK], BF16)
+        def first_layer(name, weights, w_plane, tokens, t_plane, col, banks, hidden):
             for g in range(SLOTS // GROUP):
                 acc = bank("%s_acc%d" % (name, g), banks[g])
                 cols = slice(col + g * GROUP, col + (g + 1) * GROUP)
@@ -139,65 +157,93 @@ def tile_moe_mmo_silu_kernel(
             nc.vector.quantize_mx(codes[:].bitcast(FP8X4), plane[:], hidden[:])
             return codes, plane
 
-        def second_matmul(acc, e, b, hidden):
+        def second_matmul(acc, e, b, hidden, cols=slice(0, SLOTS)):
             codes, plane = hidden
             nc.tensor.matmul_mx(
                 acc,
                 lhsT=w2_codes[:, e, 2 * P * b : 2 * P * (b + 1)].bitcast(FP4X4),
                 lhsT_scale=w2_plane[:, e, P * b : P * (b + 1)],
-                rhs=codes[:].bitcast(FP8X4), rhs_scale=plane[:],
+                rhs=codes[:, cols].bitcast(FP8X4), rhs_scale=plane[:, cols],
                 start=True, stop=True,
             )
 
-        def text_block(e, b, hidden, bank_no, tag=None):
-            acc = bank("text_acc%d_%d" % (e, b), bank_no)
-            second_matmul(acc[:, 0:SLOTS], e, b, hidden)
-            staged = sb("text_staged%d_%d" % (e, b), [P, SLOTS], F32, tag)
-            nc.scalar.copy(staged[:], acc[:, 0:SLOTS])
+        def result_block(side, e, b, hidden, bank_no, first=0, count=SLOTS, staged=None):
+            windows, offsets, gate, column = side
+            name = "%d_%d_%d_%d" % (column, e, b, first)
+            acc = bank("acc2_" + name, bank_no)
+            second_matmul(acc[:, 0:count], e, b, hidden, slice(first, first + count))
+            if staged is None:
+                staged = sb("staged" + name, [P, count], F32)[:]
+            nc.scalar.copy(staged, acc[:, 0:count])
+            slot = e * SLOTS + first
             nc.vector.tensor_tensor(
-                text_out[b][:].indirect(text_list[:, e * LIST_COLS : (e + 1) * LIST_COLS]),
-                staged[:], g1[:, e * SLOTS : (e + 1) * SLOTS], MULT,
+                windows[b][:].indirect(offsets[:, slot // 16 : (slot + count) // 16]),
+                staged, gate[:, slot : slot + count], MULT,
             )
             if e == E - 1:
-                nc.sync.dma_start(out[b * P : (b + 1) * P, 0:T], text_out[b][:])
+                width = windows[b].shape[1]
+                nc.sync.dma_start(out[b * P : (b + 1) * P, column : column + width], windows[b][:])
 
-        def patch_block(b, hidden, bank_no):
-            acc = bank("patch_acc%d" % b, bank_no)
-            for e in range(E):
-                second_matmul(acc[:, e * SLOTS : (e + 1) * SLOTS], e, b, hidden[e])
-            staged = sb("patch_staged%d" % b, [P, E * SLOTS], F32)
-            nc.scalar.copy(staged[:], acc[:])
-            window = patch_out[b % PATCH_WINDOWS]
-            nc.vector.tensor_tensor(window[:].indirect(patch_list[:]), staged[:], g2[:], MULT)
-            nc.sync.dma_start(out[b * P : (b + 1) * P, T : T + Q], window[:])
-
-        def quantize_wz(e):
-            grouped = sb("wz_grouped%d" % e, [P, H * PACK], BF16)
+        def round_wz(e, grouped, half):
+            ms = slice(half * P // 2, (half + 1) * P // 2)
             nc.scalar.copy(
-                grouped[:].rearrange("p (t m j) -> p m t j", t=PACK, j=PACK),
-                wz_raw[e][:].rearrange("p j (m t) -> p m t j", t=PACK),
+                grouped[:].rearrange("p (t m j) -> p m t j", t=PACK, j=PACK)[:, ms],
+                wz_raw[e][half][:].rearrange("p j (m t) -> p m t j", t=PACK),
             )
+
+        def quantize_wz(e, grouped):
             codes = sb("wz_codes%d" % e, [P, H], U32)
             plane = sb("wz_plane%d" % e, [P, H], U8)
             nc.vector.quantize_mx(codes[:].bitcast(FP8X4), plane[:], grouped[:])
             return (lambda t: codes[:, P * t : P * (t + 1)].bitcast(FP8X4)), plane
 
-        text_hidden = []
-        for e in range(E):
-            tokens, t_plane = gather("x%d" % e, x_win, xs_win, text_list[:, e * LIST_COLS : (e + 1) * LIST_COLS], SLOTS)
-            weights, w_plane = permute_w1(e)
-            text_hidden.append(first_layer("text%d" % e, weights, w_plane, tokens, t_plane, 0, (2 * e, 2 * e + 1)))
+        text = (text_out, text_list, g1, 0)
+        patch = (patch_out, patch_list, g2, T)
+        text_tokens = [
+            gather("x%d" % e, x_win, xs_win, text_list[:, e * LIST_COLS : (e + 1) * LIST_COLS], SLOTS) for e in range(E)
+        ]
         patches, p_plane = gather("z", z_win, zs_win, patch_list[:], E * SLOTS)
-        for b in range(BLOCKS):
-            text_block(0, b, text_hidden[0], 4 + b)
-        text_block(1, 0, text_hidden[1], 0)
-        wz_q = [quantize_wz(e) for e in range(E)]
-        text_block(1, 1, text_hidden[1], 1, "wz_raw0")
-        patch_hidden = [
-            first_layer("patch%d" % e, wz_q[e][0], wz_q[e][1], patches, p_plane, e * SLOTS, (2 + 2 * e, 3 + 2 * e))
+        text_hidden = [
+            (sb("text_hcodes%d" % e, [P, SLOTS], U32, "z_win" if e == 0 else None), sb("text_hplane%d" % e, [P, SLOTS], U8))
             for e in range(E)
         ]
-        text_block(1, 2, text_hidden[1], 2)
+        for g in range(2):
+            hidden = sb("text_hidden0_%d" % g, [P, GROUP * PACK], BF16)
+            text_first_layer(0, g, text_tokens[0][0], text_tokens[0][1], hidden[:], g, 4 + g)
+            cols = slice(g * GROUP, (g + 1) * GROUP)
+            nc.vector.quantize_mx(text_hidden[0][0][:, cols].bitcast(FP8X4), text_hidden[0][1][:, cols], hidden[:])
+            result_block(text, 0, 0, text_hidden[0], g, g * GROUP, GROUP)
+            result_block(text, 0, 1, text_hidden[0], 2 + g, g * GROUP, GROUP)
+        result_block(text, 0, 2, text_hidden[0], 6)
+        hidden = sb("text_hidden1", [P, SLOTS * PACK], BF16)
+        for g in range(2):
+            text_first_layer(
+                1, g, text_tokens[1][0], text_tokens[1][1], hidden[:, g * GROUP * PACK : (g + 1) * GROUP * PACK], 2 * g, 4 + g
+            )
+        nc.vector.quantize_mx(text_hidden[1][0][:].bitcast(FP8X4), text_hidden[1][1][:], hidden[:])
+        spare = sb("spare", [P, SLOTS], F32, "text_by_slot1_1")
+        result_block(text, 0, 3, text_hidden[0], 7, staged=spare[:])
+
+        grouped = [sb("wz_grouped%d" % e, [P, H * PACK], BF16) for e in range(E)]
+        for half in range(2):
+            round_wz(0, grouped[0], half)
+        weights, w_plane = quantize_wz(0, grouped[0])
+        spare = sb("spare", [P, 2 * SLOTS], F32, "wz_raw0_1")
+        for b in range(2):
+            result_block(text, 1, b, text_hidden[1], 7 - b, staged=spare[:, b * SLOTS : (b + 1) * SLOTS])
+        round_wz(1, grouped[1], 0)
+        hidden = sb("patch_hidden0", [P, SLOTS * PACK], BF16, "wz_raw1_0")
+        patch_hidden0 = first_layer("patch0", weights, w_plane, patches, p_plane, 0, (0, 1), hidden)
+        result_block(text, 1, 2, text_hidden[1], 0)
+        round_wz(1, grouped[1], 1)
+        weights, w_plane = quantize_wz(1, grouped[1])
+        spare = sb("spare", [P, 2 * SLOTS], F32, "wz_raw1_1")
+        for b in range(2):
+            result_block(patch, 0, b, patch_hidden0, 2 + b, staged=spare[:, b * SLOTS : (b + 1) * SLOTS])
+        hidden = sb("patch_hidden1", [P, SLOTS * PACK], BF16)
+        patch_hidden1 = first_layer("patch1", weights, w_plane, patches, p_plane, SLOTS, (4, 5), hidden)
+        for b in range(2, BLOCKS):
+            result_block(patch, 0, b, patch_hidden0, 2 + b)
         for b in range(BLOCKS):
-            patch_block(b, patch_hidden, (6, 7, 0, 1)[b])
-        text_block(1, 3, text_hidden[1], 1)
+            result_block(patch, 1, b, patch_hidden1, (6, 7, 1, 2)[b])
+        result_block(text, 1, 3, text_hidden[1], 2)

from contextlib import ExitStack

import concourse.mybir as mybir
from concourse.masks import make_identity

F32 = mybir.dt.float32
BF16 = mybir.dt.bfloat16
I32 = mybir.dt.int32
U32 = mybir.dt.uint32
U16 = mybir.dt.uint16
U8 = mybir.dt.uint8
FP8X4 = mybir.dt.float8_e4m3fn_x4
FP4X4 = mybir.dt.float4_e2m1fn_x4
SILU = mybir.ActivationFunctionType.Silu
MULT = mybir.AluOpType.mult

P = 128
PACK = 4
E = 2
SLOTS = 256
T = 512
Q = 1024
H = 512
N = 512
GROUP = 128
BLOCKS = N // P
LIST_COLS = SLOTS // 16

FLOPS = 1073741824


def tile_moe_mmo_silu_kernel(
    tc, x_words, x_scales, z_words, z_scales, w1_words, w1_scales, wz, w2_words, w2_scales,
    gate1, gate2, offs, offs2, out,
):
    nc = tc.nc
    with ExitStack() as ctx:
        keep = ctx.enter_context(tc.tile_pool(name="keep", bufs=1))
        psum = ctx.enter_context(tc.psum_pool(name="psum", bufs=1))

        def sb(name, shape, dtype, tag=None):
            return keep.tile(shape, dtype, name=name, tag=tag or name, align_bytes=64)

        def bank(name, b):
            return psum.tile([P, 512], F32, name=name, tag="bank%d" % b)

        text_list = keep.tile([P, T // 16], U16, name="text_list")
        patch_list = keep.tile([P, T // 16], U16, name="patch_list")
        x_win = sb("x_win", [P, T], I32)
        z_win = sb("z_win", [P, Q], I32)
        xs_win = sb("xs_win", [P, T], U8)
        zs_win = sb("zs_win", [P, Q], U8)
        w1_raw = sb("w1_raw", [P, E, 2 * H], U8)
        w1s_raw = sb("w1s_raw", [P, E, H], U8)
        w2_codes = sb("w2_codes", [P, E, 2 * N], U8)
        w2_plane = sb("w2_plane", [P, E, N], U8)
        g1 = sb("g1", [P, E * SLOTS], F32)
        g2 = sb("g2", [P, E * SLOTS], F32)
        wz_raw = [[sb("wz_raw%d_%d" % (e, h), [P, PACK, H // 2], F32) for h in range(2)] for e in range(E)]
        text_out = [sb("text_out%d" % b, [P, T], F32) for b in range(BLOCKS)]
        patch_out = [sb("patch_out%d" % b, [P, Q], F32) for b in range(BLOCKS)]

        nc.vector.memset(xs_win[:].bitcast(I32), 0)
        nc.vector.memset(w1s_raw[:].rearrange("p e c -> p (e c)").bitcast(I32), 0)
        nc.vector.memset(zs_win[:].bitcast(I32), 0)
        nc.vector.memset(w2_plane[:].rearrange("p e c -> p (e c)").bitcast(I32), 0)
        warm = sb("warm", [P, 2], F32)
        nc.vector.memset(warm[:, 0:1], 0.0)
        nc.scalar.activation(warm[:, 1:2], warm[:, 0:1], SILU)
        identity = sb("identity", [P, P], F32)
        make_identity(nc, identity[:])
        for b in range(BLOCKS):
            nc.gpsimd.memset(patch_out[b][:], 0.0)

        def load_token_scales(plane, scales):
            rows = scales[0].rearrange("(q r) t -> r q t", r=4)
            for r in range(4):
                nc.sync.dma_start(plane[r:P:32, :].bitcast(I32), rows[r].bitcast(I32))

        def load_weight_scales(plane, scales):
            rows = scales.rearrange("e s (q r) c -> r q (e s) c", r=4)
            for r in range(4):
                nc.sync.dma_start(plane[r:P:32, :, :].bitcast(I32), rows[r].bitcast(I32))

        def load_weight_words(tile, words):
            nc.sync.dma_start(tile[:].bitcast(I32), words.rearrange("e s p b -> p (e s) b").bitcast(I32))

        def load_token_words(tile, words):
            nc.sync.dma_start(tile[:], words[0].rearrange("p t d -> p (t d)").bitcast(I32))

        nc.sync.dma_start(text_list[:], offs)
        load_token_words(x_win, x_words)
        load_token_scales(xs_win, x_scales)
        load_weight_words(w1_raw, w1_words)
        load_weight_scales(w1s_raw, w1_scales)
        nc.sync.dma_start(patch_list[:], offs2)
        load_token_words(z_win, z_words)
        load_token_scales(zs_win, z_scales)
        load_weight_scales(w2_plane, w2_scales)
        load_weight_words(w2_codes, w2_words)
        nc.sync.dma_start(g1[:], gate1)
        for e in range(E):
            for h in range(2):
                nc.sync.dma_start(
                    wz_raw[e][h][:], wz[e][:, h * H // 2 : (h + 1) * H // 2].rearrange("(p j) c -> p j c", j=PACK)
                )
        nc.sync.dma_start(g2[:], gate2)

        def gather(name, words, plane, offsets, count):
            got = sb(name + "_words", [P, count], U32)
            got_plane = sb(name + "_plane", [P, count], U8)
            nc.vector.tensor_copy(got[:], words[:].bitcast(U32).indirect(offsets))
            nc.vector.tensor_copy(got_plane[:], plane[:].indirect(offsets))
            return got, got_plane

        def text_first_layer(e, g, tokens, t_plane, hidden, acc_bank, turn_bank):
            cols = slice(g * GROUP, (g + 1) * GROUP)
            acc = bank("text_acc1_%d_%d" % (e, g), acc_bank)
            nc.tensor.matmul_mx(
                acc[:],
                lhsT=tokens[:, cols].bitcast(FP8X4), lhsT_scale=t_plane[:, cols],
                rhs=w1_raw[:, e, :].bitcast(FP4X4), rhs_scale=w1s_raw[:, e, :],
                start=True, stop=True,
            )
            by_slot = sb("text_by_slot%d_%d" % (e, g), [P, H], BF16)
            nc.scalar.activation(
                by_slot[:].rearrange("s (u p b) -> s u p b", u=2, b=2),
                acc[:].rearrange("s (p u b) -> s u p b", u=2, b=2), SILU,
            )
            turned = bank("text_turned%d_%d" % (e, g), turn_bank)
            for u in range(2):
                nc.tensor.transpose(
                    turned[:, u * P : (u + 1) * P], by_slot[:].bitcast(F32)[:, u * P : (u + 1) * P], identity[:]
                )
            nc.scalar.copy(
                hidden.bitcast(F32).rearrange("p (s u) -> p s u", u=2),
                turned[:, 0 : 2 * P].rearrange("p (u s) -> p s u", u=2),
            )

        def first_layer(name, weights, w_plane, tokens, t_plane, col, banks, hidden):
            for g in range(SLOTS // GROUP):
                acc = bank("%s_acc%d" % (name, g), banks[g])
                cols = slice(col + g * GROUP, col + (g + 1) * GROUP)
                for t in range(PACK):
                    nc.tensor.matmul_mx(
                        acc[:, t * GROUP : (t + 1) * GROUP],
                        lhsT=weights(t), lhsT_scale=w_plane[:, t * P : (t + 1) * P],
                        rhs=tokens[:, cols].bitcast(FP8X4), rhs_scale=t_plane[:, cols],
                        start=True, stop=True,
                    )
                nc.scalar.activation(
                    hidden[:, g * GROUP * PACK : (g + 1) * GROUP * PACK].rearrange("p (n t) -> p n t", t=PACK),
                    acc[:].rearrange("p (t n) -> p n t", t=PACK), SILU,
                )
            codes = sb(name + "_hcodes", [P, SLOTS], U32)
            plane = sb(name + "_hplane", [P, SLOTS], U8)
            nc.vector.quantize_mx(codes[:].bitcast(FP8X4), plane[:], hidden[:])
            return codes, plane

        def second_matmul(acc, e, b, hidden, cols=slice(0, SLOTS)):
            codes, plane = hidden
            nc.tensor.matmul_mx(
                acc,
                lhsT=w2_codes[:, e, 2 * P * b : 2 * P * (b + 1)].bitcast(FP4X4),
                lhsT_scale=w2_plane[:, e, P * b : P * (b + 1)],
                rhs=codes[:, cols].bitcast(FP8X4), rhs_scale=plane[:, cols],
                start=True, stop=True,
            )

        def result_block(side, e, b, hidden, bank_no, first=0, count=SLOTS, staged=None):
            windows, offsets, gate, column = side
            name = "%d_%d_%d_%d" % (column, e, b, first)
            acc = bank("acc2_" + name, bank_no)
            second_matmul(acc[:, 0:count], e, b, hidden, slice(first, first + count))
            if staged is None:
                staged = sb("staged" + name, [P, count], F32)[:]
            nc.scalar.copy(staged, acc[:, 0:count])
            slot = e * SLOTS + first
            nc.vector.tensor_tensor(
                windows[b][:].indirect(offsets[:, slot // 16 : (slot + count) // 16]),
                staged, gate[:, slot : slot + count], MULT,
            )
            if e == E - 1:
                width = windows[b].shape[1]
                nc.sync.dma_start(out[b * P : (b + 1) * P, column : column + width], windows[b][:])

        def round_wz(e, grouped, half):
            ms = slice(half * P // 2, (half + 1) * P // 2)
            nc.scalar.copy(
                grouped[:].rearrange("p (t m j) -> p m t j", t=PACK, j=PACK)[:, ms],
                wz_raw[e][half][:].rearrange("p j (m t) -> p m t j", t=PACK),
            )

        def quantize_wz(e, grouped):
            codes = sb("wz_codes%d" % e, [P, H], U32)
            plane = sb("wz_plane%d" % e, [P, H], U8)
            nc.vector.quantize_mx(codes[:].bitcast(FP8X4), plane[:], grouped[:])
            return (lambda t: codes[:, P * t : P * (t + 1)].bitcast(FP8X4)), plane

        text = (text_out, text_list, g1, 0)
        patch = (patch_out, patch_list, g2, T)
        text_tokens = [
            gather("x%d" % e, x_win, xs_win, text_list[:, e * LIST_COLS : (e + 1) * LIST_COLS], SLOTS) for e in range(E)
        ]
        patches, p_plane = gather("z", z_win, zs_win, patch_list[:], E * SLOTS)
        text_hidden = [
            (sb("text_hcodes%d" % e, [P, SLOTS], U32, "z_win" if e == 0 else None), sb("text_hplane%d" % e, [P, SLOTS], U8))
            for e in range(E)
        ]
        for g in range(2):
            hidden = sb("text_hidden0_%d" % g, [P, GROUP * PACK], BF16)
            text_first_layer(0, g, text_tokens[0][0], text_tokens[0][1], hidden[:], g, 4 + g)
            cols = slice(g * GROUP, (g + 1) * GROUP)
            nc.vector.quantize_mx(text_hidden[0][0][:, cols].bitcast(FP8X4), text_hidden[0][1][:, cols], hidden[:])
            result_block(text, 0, 0, text_hidden[0], g, g * GROUP, GROUP)
            result_block(text, 0, 1, text_hidden[0], 2 + g, g * GROUP, GROUP)
        result_block(text, 0, 2, text_hidden[0], 6)
        hidden = sb("text_hidden1", [P, SLOTS * PACK], BF16)
        for g in range(2):
            text_first_layer(
                1, g, text_tokens[1][0], text_tokens[1][1], hidden[:, g * GROUP * PACK : (g + 1) * GROUP * PACK], 2 * g, 4 + g
            )
        nc.vector.quantize_mx(text_hidden[1][0][:].bitcast(FP8X4), text_hidden[1][1][:], hidden[:])
        spare = sb("spare", [P, SLOTS], F32, "text_by_slot1_1")
        result_block(text, 0, 3, text_hidden[0], 7, staged=spare[:])

        grouped = [sb("wz_grouped%d" % e, [P, H * PACK], BF16) for e in range(E)]
        for half in range(2):
            round_wz(0, grouped[0], half)
        weights, w_plane = quantize_wz(0, grouped[0])
        spare = sb("spare", [P, 2 * SLOTS], F32, "wz_raw0_1")
        for b in range(2):
            result_block(text, 1, b, text_hidden[1], 7 - b, staged=spare[:, b * SLOTS : (b + 1) * SLOTS])
        round_wz(1, grouped[1], 0)
        hidden = sb("patch_hidden0", [P, SLOTS * PACK], BF16, "wz_raw1_0")
        patch_hidden0 = first_layer("patch0", weights, w_plane, patches, p_plane, 0, (0, 1), hidden)
        result_block(text, 1, 2, text_hidden[1], 0)
        round_wz(1, grouped[1], 1)
        weights, w_plane = quantize_wz(1, grouped[1])
        spare = sb("spare", [P, 2 * SLOTS], F32, "wz_raw1_1")
        for b in range(2):
            result_block(patch, 0, b, patch_hidden0, 2 + b, staged=spare[:, b * SLOTS : (b + 1) * SLOTS])
        hidden = sb("patch_hidden1", [P, SLOTS * PACK], BF16)
        patch_hidden1 = first_layer("patch1", weights, w_plane, patches, p_plane, SLOTS, (4, 5), hidden)
        for b in range(2, BLOCKS):
            result_block(patch, 0, b, patch_hidden0, 2 + b)
        for b in range(BLOCKS):
            result_block(patch, 1, b, patch_hidden1, (6, 7, 1, 2)[b])
        result_block(text, 1, 3, text_hidden[1], 2)
